import numpy as np
import ml_dtypes


def mxq(x, axis, fmt="e4m3"):
    dtype, down = {"e4m3": (ml_dtypes.float8_e4m3fn, 7), "e5m2": (ml_dtypes.float8_e5m2, 14)}[fmt]
    v = np.moveaxis(np.asarray(x, np.float32).astype(ml_dtypes.bfloat16).astype(np.float64), axis, -1)
    blocks = v.reshape(v.shape[:-1] + (-1, 32))
    amax = np.abs(blocks).max(-1, keepdims=True)
    byte = np.maximum(np.where(amax > 0, np.frexp(amax)[1] - 1 + 127, 0) - down, 1)
    scale = np.exp2(byte - 127.0)
    codes = (blocks / scale).astype(np.float32).astype(dtype).astype(np.float64)
    return np.moveaxis((codes * scale).reshape(v.shape), -1, axis)


WIDE = False


def mx_kscale(k, group=512):
    if not WIDE:
        return np.ones(k)
    levels = np.array([10, -10, 5, -5, 0])
    if group != 512:
        return np.exp2(np.random.permutation(np.resize(levels, k // group))).repeat(group)
    if k % 512:
        return np.exp2(np.random.permutation(np.resize(levels, k // 32))).repeat(32)
    a = np.empty((k // 512, 16))
    for p in range(k // 512):
        a[p, :8] = np.random.permutation(np.resize(levels, 8))
        for g in range(8):
            far = levels[np.abs(levels - a[p, g]) >= 10]
            a[p, g + 8] = far[np.random.randint(len(far))]
    return np.exp2(a.ravel()).repeat(32)


def f64(x):
    return np.asarray(x).astype(np.float64)


def striped(idx):
    return np.tile(np.asarray(idx).reshape(-1, 16).T, (8, 1)).astype(np.uint16)


def unstriped(offs):
    return offs[:16].T.reshape(-1).astype(np.int64)


H, KV, D, NQ, N = 2, 2, 256, 512, 1024


def setup_inputs():
    n = np.random.standard_normal
    s = mx_kscale(D, 0)[:, None]
    u = mx_kscale(N)
    t = np.random.uniform(0.5, 2.0, N) * u
    v = n((KV, N, 128))
    return {
        "qT": (n((H, D, NQ)) * s * (0.70 / np.sqrt(D))).astype(np.float32),
        "kT": (n((KV, D, N)) / s).astype(np.float32),
        "t": t.reshape(N, 1).astype(np.float32),
        "v": (v / t[:, None]).astype(np.float32),
        "mask": (np.arange(N)[:, None] <= np.sort(np.random.randint(N // 4, N, NQ))[None, :]).astype(np.float32),
        "gn": np.tile(np.random.uniform(0.5, 2.0, 128), (128, 1)).astype(np.float32),
        "og": n((H, NQ, 128)).astype(np.float32),
    }


def reference(qT, kT, t, v, mask, gn, og):
    a = mxq(f64(kT), 1, "e4m3").transpose(0, 2, 1) @ mxq(f64(qT), 1, "e4m3")
    p = np.maximum(a, 0.0)
    p = p * f64(mask)
    w = p * f64(t)
    y = mxq(w, 1, "e4m3").transpose(0, 2, 1) @ mxq(f64(v), 1, "e4m3")
    y = y / 16.0
    y = y / np.sqrt(np.mean(np.square(y), -1, keepdims=True) + 1e-5) * f64(gn)[:1]
    y = y / (1.0 + np.exp(-f64(og)))
    return y

@@ -1,0 +1,393 @@
+from contextlib import ExitStack
+
+import concourse.mybir as mybir
+
+H, D, NQ, N, E = 2, 256, 512, 1024, 128
+FLOPS = 2 * H * N * NQ * (D + E)
+
+F32 = mybir.dt.float32
+BF16 = mybir.dt.bfloat16
+U32 = mybir.dt.uint32
+U8 = mybir.dt.uint8
+FP8X4 = mybir.dt.float8_e4m3fn_x4
+ALU = mybir.AluOpType
+ACT = mybir.ActivationFunctionType
+
+P = 128
+PACK = 4
+ROWS = D // PACK
+TOK = P * PACK
+PASSES = N // TOK
+QT = 128
+TILES = NQ // QT
+HALF = TOK // 2
+SCORE_BANKS = 3
+
+
+def tile_rows_a_relu_mask_onorm_gate_kernel(tc, qT, kT, t, v, mask, gn, og, out):
+    nc = tc.nc
+    with ExitStack() as ctx:
+        sb = ctx.enter_context(tc.tile_pool(name="sb", bufs=1))
+        ps = ctx.enter_context(tc.psum_pool(name="ps", bufs=1))
+
+        def sbuf(name, shape, dtype):
+            return sb.tile(shape, dtype, name=name, align_bytes=64)
+
+        score = [[ps.tile([P, PACK, QT], F32, name="score%d_%d" % (h, b)) for b in range(SCORE_BANKS)] for h in range(H)]
+        y = [ps.tile([P, 4, E], F32, name="y%d" % b) for b in range(2)]
+
+        t_sb = sbuf("t_sb", [P, PASSES, PACK], F32)
+        gn_sb = sbuf("gn_sb", [P, E], F32)
+        q_groups = [(0, 1), (1, 1), (2, 2)]
+        q_raw = {u0: sbuf("q_raw%d" % u0, [P, PACK, n * QT], F32) for u0, n in q_groups}
+        k_raw = [[sbuf("k_raw%d_%d" % (c, a), [P, PACK, HALF], F32) for a in range(2)] for c in range(PASSES)]
+        m_groups = [(0, 0, 1), (0, 1, 1), (0, 2, 1), (0, 3, 1), (1, 0, 2), (1, 2, 1), (1, 3, 1)]
+        m_raw = {(c, u0): sbuf("m_raw%d_%d" % (c, u0), [P, PACK, n * QT], F32) for c, u0, n in m_groups}
+        v_raw = [sbuf("v_raw%d" % h, [P, PASSES, PACK, E], F32) for h in range(H)]
+        og_sb = [sbuf("og_sb%d" % a, [P, H, 2, E], F32) for a in range(2)]
+
+        q_bf = sbuf("q_bf", [P, NQ, PACK], BF16)
+        q_codes = sbuf("q_codes", [P, NQ], U32)
+        q_scales = sbuf("q_scales", [P, NQ], U8)
+        k0_bf = [sbuf("k0_bf%d" % a, [P, PACK, P // 2, PACK], BF16) for a in range(2)]
+        k1_bf = sbuf("k1_bf", [P, PACK, P, PACK], BF16)
+        k_codes = [sbuf("k_codes%d" % c, [P, PACK, P], U32) for c in range(PASSES)]
+        k_scales = [sbuf("k_scales%d" % c, [P, PACK, P], U8) for c in range(PASSES)]
+        v_bf = [sbuf("v_bf%d" % h, [P, PASSES, E, PACK], BF16) for h in range(H)]
+        v_codes = [sbuf("v_codes%d" % h, [P, PASSES, E], U32) for h in range(H)]
+        v_scales = [sbuf("v_scales%d" % h, [P, PASSES, E], U8) for h in range(H)]
+        mt = [[sbuf("mt%d_%d" % (c, u), [P, QT * PACK], F32) for u in range(TILES)] for c in range(PASSES)]
+        w_bf = [sbuf("w_bf%d" % c, [P, TILES * H, QT, PACK], BF16) for c in range(PASSES)]
+        w_codes = [sbuf("w_codes%d" % c, [P, TILES * H, QT], U32) for c in range(PASSES)]
+        w_scales = [sbuf("w_scales%d" % c, [P, TILES * H, QT], U8) for c in range(PASSES)]
+        sig = [sbuf("sig%d" % a, [P, H, 2, E], F32) for a in range(2)]
+        gate = [sbuf("gate%d" % u, [P, H, E], F32) for u in range(TILES)]
+        squares = sbuf("squares", [P, E], BF16)
+        ssq = [sbuf("ssq%d" % u, [P, H], F32) for u in range(TILES)]
+        msq = [sbuf("msq%d" % u, [P, H], F32) for u in range(TILES)]
+        rstd = [sbuf("rstd%d" % u, [P, H], F32) for u in range(TILES)]
+        res = [sbuf("res%d" % u, [P, H, E], F32) for u in range(TILES)]
+        minus_half = sbuf("minus_half", [P, H], F32)
+        warm = sbuf("warm", [P, 8], F32)
+        warm2 = sbuf("warm2", [P, 8], F32)
+
+        q_hbm = qT.rearrange("h (p j) q -> (h p) j q", j=PACK)
+        k_hbm = kT.rearrange("h (p j) i -> (h p) j i", j=PACK)
+        m_hbm = mask.rearrange("(c p r) q -> c p r q", c=PASSES, r=PACK)
+
+        def load_q(u0):
+            n = q_raw[u0].shape[2]
+            nc.sync.dma_start(out=q_raw[u0][:], in_=q_hbm[:, :, u0 * QT : u0 * QT + n])
+
+        def load_k(c, a):
+            i0 = c * TOK + a * HALF
+            nc.sync.dma_start(out=k_raw[c][a][:], in_=k_hbm[:, :, i0 : i0 + HALF])
+
+        def load_m(c, u0):
+            n = m_raw[(c, u0)].shape[2]
+            nc.sync.dma_start(out=m_raw[(c, u0)][:], in_=m_hbm[c][:, :, u0 * QT : u0 * QT + n])
+
+        def load_v(h):
+            nc.sync.dma_start(
+                out=v_raw[h][:].rearrange("p c r e -> p c (r e)"),
+                in_=v[h].rearrange("(c p r) e -> p c (r e)", c=PASSES, r=PACK),
+            )
+
+        def load_og(a):
+            for h in range(H):
+                nc.sync.dma_start(
+                    out=og_sb[a][:, h, :, :],
+                    in_=og[h][a * 2 * QT : (a + 1) * 2 * QT, :].rearrange("(u p) e -> p u e", p=P),
+                )
+
+        def cast(eng, dst, src):
+            if eng == "V":
+                nc.vector.tensor_copy(out=dst, in_=src)
+            else:
+                nc.scalar.copy(out=dst, in_=src)
+
+        def pack_q(eng, u):
+            u0 = min(u, 2)
+            src = q_raw[u0][:, :, (u - u0) * QT : (u - u0 + 1) * QT]
+            dst = q_bf[:, u * QT : (u + 1) * QT, :]
+            cast(eng, dst.rearrange("p (g i) j -> p g j i", i=4), src.rearrange("p j (g i) -> p g j i", i=4))
+
+        def pack_k(eng, c, a, r0, r1):
+            src = k_raw[c][a][:].rearrange("p j (s r) -> p s r j", r=PACK)[:, :, r0:r1, :]
+            if c == 0:
+                dst = k0_bf[a][:, r0:r1, :, :]
+            else:
+                dst = k1_bf[:, r0:r1, a * 64 : (a + 1) * 64, :]
+            cast(eng, dst.rearrange("p r s j -> p s r j"), src)
+
+        def pack_v(eng, h, c):
+            src = v_raw[h][:, c, :, :]
+            dst = v_bf[h][:, c, :, :]
+            cast(eng, dst.rearrange("p (g i) r -> p g r i", i=4), src.rearrange("p r (g i) -> p g r i", i=4))
+
+        def quant(codes, scales, src):
+            nc.vector.quantize_mx(out=codes.bitcast(FP8X4), scales=scales, in_=src)
+
+        def quant_q(u0, u1):
+            cols = slice(u0 * QT, u1 * QT)
+            quant(q_codes[:, cols], q_scales[:, cols], q_bf[:, cols, :].rearrange("p q j -> p (q j)"))
+
+        def quant_k0(a, r):
+            cols = slice(a * 64, (a + 1) * 64)
+            quant(k_codes[0][:, r, cols], k_scales[0][:, r, cols], k0_bf[a][:, r, :, :].rearrange("p s j -> p (s j)"))
+
+        def quant_k1(r0, r1):
+            quant(
+                k_codes[1][:, r0:r1, :].rearrange("p r s -> p (r s)"),
+                k_scales[1][:, r0:r1, :].rearrange("p r s -> p (r s)"),
+                k1_bf[:, r0:r1, :, :].rearrange("p r s j -> p (r s j)"),
+            )
+
+        def quant_v(h):
+            quant(
+                v_codes[h][:].rearrange("p c e -> p (c e)"),
+                v_scales[h][:].rearrange("p c e -> p (c e)"),
+                v_bf[h][:].rearrange("p c e r -> p (c e r)"),
+            )
+
+        def quant_w(c, x0, x1):
+            quant(
+                w_codes[c][:, x0:x1, :].rearrange("p x m -> p (x m)"),
+                w_scales[c][:, x0:x1, :].rearrange("p x m -> p (x m)"),
+                w_bf[c][:, x0:x1, :, :].rearrange("p x m r -> p (x m r)"),
+            )
+
+        interleaved = {}
+
+        def prep(eng, c, u, m0=0, m1=QT):
+            u0 = max(g[1] for g in m_groups if g[0] == c and g[1] <= u)
+            src = m_raw[(c, u0)][:, :, (u - u0) * QT + m0 : (u - u0) * QT + m1]
+            if eng == "S":
+                interleaved[(c, u)] = False
+                dst = mt[c][u][:].rearrange("p (r m) -> p r m", r=PACK)
+                for r in range(PACK):
+                    nc.scalar.activation(out=dst[:, r, m0:m1], in_=src[:, r, :], func=ACT.Copy, scale=t_sb[:, c, r : r + 1])
+            else:
+                interleaved[(c, u)] = True
+                dst = mt[c][u][:].rearrange("p (m r) -> p m r", r=PACK)[:, m0:m1, :]
+                e = nc.vector if eng == "V" else nc.gpsimd
+                e.tensor_tensor(
+                    out=dst,
+                    in0=src.rearrange("p r m -> p m r"),
+                    in1=t_sb[:, c, :].unsqueeze(1).to_broadcast([P, m1 - m0, PACK]),
+                    op=ALU.mult,
+                )
+
+        def scores(c, u):
+            b = (c * TILES + u) % SCORE_BANKS
+            for r in range(PACK):
+                for h in range(H):
+                    rows = slice(h * ROWS, (h + 1) * ROWS)
+                    cols = slice(u * QT, (u + 1) * QT)
+                    nc.tensor.matmul_mx(
+                        out=score[h][b][:, r, :],
+                        lhsT=k_codes[c][rows, r, :].bitcast(FP8X4),
+                        lhsT_scale=k_scales[c][rows, r, :],
+                        rhs=q_codes[rows, cols].bitcast(FP8X4),
+                        rhs_scale=q_scales[rows, cols],
+                        start=True,
+                        stop=True,
+                    )
+
+        def weigh(c, u, h):
+            b = (c * TILES + u) % SCORE_BANKS
+            if interleaved[(c, u)]:
+                f = mt[c][u][:].rearrange("p (m r) -> p m r", r=PACK)
+            else:
+                f = mt[c][u][:].rearrange("p (r m) -> p m r", r=PACK)
+            nc.vector.scalar_tensor_tensor(
+                out=w_bf[c][:, u * H + h, :, :],
+                in0=score[h][b][:].rearrange("p r m -> p m r"),
+                scalar=0.0,
+                in1=f,
+                op0=ALU.max,
+                op1=ALU.mult,
+            )
+
+        def y_of(u, h):
+            return y[u % 2][:, (u // 2) * H + h, :]
+
+        def values(u, h):
+            for c in range(PASSES):
+                nc.tensor.matmul_mx(
+                    out=y_of(u, h),
+                    lhsT=w_codes[c][:, u * H + h, :].bitcast(FP8X4),
+                    lhsT_scale=w_scales[c][:, u * H + h, :],
+                    rhs=v_codes[h][:, c, :].bitcast(FP8X4),
+                    rhs_scale=v_scales[h][:, c, :],
+                    start=(c == 0),
+                    stop=(c == PASSES - 1),
+                )
+
+        def sigmoid(a):
+            nc.scalar.activation(out=sig[a][:], in_=og_sb[a][:], func=ACT.Sigmoid)
+
+        def make_gate(eng, u):
+            e = nc.vector if eng == "V" else nc.gpsimd
+            e.tensor_tensor(
+                out=gate[u][:],
+                in0=sig[u // 2][:, :, u % 2, :],
+                in1=gn_sb[:].unsqueeze(1).to_broadcast([P, H, E]),
+                op=ALU.mult,
+            )
+
+        def square(u, h):
+            nc.scalar.activation(out=squares[:], in_=y_of(u, h), func=ACT.Square, accum_out=ssq[u][:, h : h + 1])
+
+        def norm(u, h0, h1):
+            nc.gpsimd.tensor_scalar(
+                out=msq[u][:, h0:h1], in0=ssq[u][:, h0:h1], scalar1=1.0 / E, scalar2=256.0 * 1e-5, op0=ALU.mult, op1=ALU.add
+            )
+            nc.gpsimd.tensor_tensor(out=rstd[u][:, h0:h1], in0=msq[u][:, h0:h1], in1=minus_half[:, h0:h1], op=ALU.pow)
+
+        def finish(u, h):
+            nc.vector.scalar_tensor_tensor(
+                out=res[u][:, h, :],
+                in0=y_of(u, h),
+                scalar=rstd[u][:, h : h + 1],
+                in1=gate[u][:, h, :],
+                op0=ALU.mult,
+                op1=ALU.mult,
+            )
+
+        def store(u, h0, h1):
+            nc.sync.dma_start(
+                out=out[h0:h1, u * QT : (u + 1) * QT, :].rearrange("h p e -> p h e"),
+                in_=res[u][:, h0:h1, :],
+            )
+
+        ctx.enter_context(tc.manual_schedule())
+        nc.scalar.dma_start(out=t_sb[:], in_=t.rearrange("(c p r) o -> p c (r o)", c=PASSES, r=PACK))
+        nc.vector.memset(warm[:], 0.0)
+        nc.scalar.activation(out=warm2[:], in_=warm[:], func=ACT.Sigmoid)
+        nc.gpsimd.memset(minus_half[:], -0.5)
+        load_k(0, 0)
+        load_q(0)
+        load_k(0, 1)
+        load_m(0, 0)
+        load_q(1)
+        load_m(0, 1)
+        load_q(2)
+        load_m(0, 2)
+        load_k(1, 0)
+        load_m(0, 3)
+        load_k(1, 1)
+        load_m(1, 0)
+        load_v(0)
+        load_m(1, 2)
+        load_v(1)
+        load_m(1, 3)
+        nc.sync.dma_start(out=gn_sb[:], in_=gn)
+        load_og(0)
+        load_og(1)
+        pack_k("V", 0, 0, 0, 4)
+        pack_q("S", 0)
+        quant_k0(0, 0)
+        quant_k0(0, 1)
+        quant_k0(0, 2)
+        quant_k0(0, 3)
+        quant_q(0, 1)
+        pack_k("V", 0, 1, 0, 2)
+        pack_k("S", 0, 1, 2, 4)
+        quant_k0(1, 0)
+        quant_k0(1, 1)
+        quant_k0(1, 2)
+        quant_k0(1, 3)
+        scores(0, 0)
+        prep("V", 0, 0)
+        pack_q("S", 1)
+        prep("G", 0, 1)
+        weigh(0, 0, 0)
+        quant_q(1, 2)
+        scores(0, 1)
+        weigh(0, 0, 1)
+        pack_q("S", 2)
+        pack_q("S", 3)
+        prep("G", 0, 2)
+        weigh(0, 1, 0)
+        quant_q(2, 4)
+        scores(0, 2)
+        weigh(0, 1, 1)
+        scores(0, 3)
+        pack_k("S", 1, 0, 0, 4)
+        prep("G", 0, 3)
+        weigh(0, 2, 0)
+        quant_w(0, 0, 4)
+        weigh(0, 2, 1)
+        pack_k("S", 1, 1, 0, 4)
+        prep("G", 1, 0)
+        weigh(0, 3, 0)
+        weigh(0, 3, 1)
+        quant_k1(0, 2)
+        quant_k1(2, 4)
+        scores(1, 0)
+        scores(1, 1)
+        quant_w(0, 4, 8)
+        prep("G", 1, 1)
+        pack_v("S", 0, 0)
+        pack_v("S", 0, 1)
+        weigh(1, 0, 0)
+        weigh(1, 0, 1)
+        scores(1, 2)
+        prep("G", 1, 2)
+        pack_v("S", 1, 0)
+        pack_v("S", 1, 1)
+        weigh(1, 1, 0)
+        quant_w(1, 0, 2)
+        weigh(1, 1, 1)
+        scores(1, 3)
+        quant_v(0)
+        prep("G", 1, 3)
+        weigh(1, 2, 0)
+        quant_w(1, 2, 4)
+        quant_v(1)
+        values(0, 0)
+        values(0, 1)
+        values(1, 0)
+        values(1, 1)
+        weigh(1, 2, 1)
+        sigmoid(0)
+        square(0, 0)
+        square(0, 1)
+        square(1, 0)
+        square(1, 1)
+        make_gate("G", 0)
+        norm(0, 0, 2)
+        make_gate("G", 1)
+        norm(1, 0, 2)
+        sigmoid(1)
+        weigh(1, 3, 0)
+        quant_w(1, 4, 6)
+        values(2, 0)
+        values(2, 1)
+        weigh(1, 3, 1)
+        quant_w(1, 6, 7)
+        values(3, 0)
+        quant_w(1, 7, 8)
+        values(3, 1)
+        square(2, 0)
+        square(2, 1)
+        finish(0, 0)
+        finish(0, 1)
+        store(0, 0, 2)
+        make_gate("G", 2)
+        norm(2, 0, 2)
+        make_gate("G", 3)
+        square(3, 0)
+        norm(3, 0, 1)
+        square(3, 1)
+        norm(3, 1, 2)
+        finish(1, 0)
+        finish(1, 1)
+        store(1, 0, 2)
+        finish(2, 0)
+        finish(2, 1)
+        store(2, 0, 2)
+        finish(3, 0)
+        finish(3, 1)
+        store(3, 0, 2)

@@ -41,7 +41,7 @@ def tile_rows_a_relu_mask_onorm_gate_kernel(tc, qT, kT, t, v, mask, gn, og, out)
         q_groups = [(0, 1), (1, 1), (2, 2)]
         q_raw = {u0: sbuf("q_raw%d" % u0, [P, PACK, n * QT], F32) for u0, n in q_groups}
         k_raw = [[sbuf("k_raw%d_%d" % (c, a), [P, PACK, HALF], F32) for a in range(2)] for c in range(PASSES)]
-        m_groups = [(0, 0, 1), (0, 1, 1), (0, 2, 1), (0, 3, 1), (1, 0, 2), (1, 2, 1), (1, 3, 1)]
+        m_groups = [(0, 0, 1), (0, 1, 1), (0, 2, 2), (1, 0, 2), (1, 2, 2)]
         m_raw = {(c, u0): sbuf("m_raw%d_%d" % (c, u0), [P, PACK, n * QT], F32) for c, u0, n in m_groups}
         v_raw = [sbuf("v_raw%d" % h, [P, PASSES, PACK, E], F32) for h in range(H)]
         og_sb = [sbuf("og_sb%d" % a, [P, H, 2, E], F32) for a in range(2)]
@@ -56,18 +56,16 @@ def tile_rows_a_relu_mask_onorm_gate_kernel(tc, qT, kT, t, v, mask, gn, og, out)
         v_bf = [sbuf("v_bf%d" % h, [P, PASSES, E, PACK], BF16) for h in range(H)]
         v_codes = [sbuf("v_codes%d" % h, [P, PASSES, E], U32) for h in range(H)]
         v_scales = [sbuf("v_scales%d" % h, [P, PASSES, E], U8) for h in range(H)]
-        mt = [[sbuf("mt%d_%d" % (c, u), [P, QT * PACK], F32) for u in range(TILES)] for c in range(PASSES)]
+        mt = {(c, u0): sbuf("mt%d_%d" % (c, u0), [P, PACK, n * QT], F32) for c, u0, n in m_groups}
         w_bf = [sbuf("w_bf%d" % c, [P, TILES * H, QT, PACK], BF16) for c in range(PASSES)]
         w_codes = [sbuf("w_codes%d" % c, [P, TILES * H, QT], U32) for c in range(PASSES)]
         w_scales = [sbuf("w_scales%d" % c, [P, TILES * H, QT], U8) for c in range(PASSES)]
         sig = [sbuf("sig%d" % a, [P, H, 2, E], F32) for a in range(2)]
         gate = [sbuf("gate%d" % u, [P, H, E], F32) for u in range(TILES)]
-        squares = sbuf("squares", [P, E], BF16)
+        squares = sbuf("squares", [P, TILES * H, E], BF16)
         ssq = [sbuf("ssq%d" % u, [P, H], F32) for u in range(TILES)]
-        msq = [sbuf("msq%d" % u, [P, H], F32) for u in range(TILES)]
         rstd = [sbuf("rstd%d" % u, [P, H], F32) for u in range(TILES)]
         res = [sbuf("res%d" % u, [P, H, E], F32) for u in range(TILES)]
-        minus_half = sbuf("minus_half", [P, H], F32)
         warm = sbuf("warm", [P, 8], F32)
         warm2 = sbuf("warm2", [P, 8], F32)
 
@@ -103,8 +101,10 @@ def tile_rows_a_relu_mask_onorm_gate_kernel(tc, qT, kT, t, v, mask, gn, og, out)
         def cast(eng, dst, src):
             if eng == "V":
                 nc.vector.tensor_copy(out=dst, in_=src)
-            else:
+            elif eng == "S":
                 nc.scalar.copy(out=dst, in_=src)
+            else:
+                nc.gpsimd.tensor_scalar(out=dst, in0=src, scalar1=1.0, scalar2=0.0, op0=ALU.mult, op1=ALU.add)
 
         def pack_q(eng, u):
             u0 = min(u, 2)
@@ -157,26 +157,26 @@ def tile_rows_a_relu_mask_onorm_gate_kernel(tc, qT, kT, t, v, mask, gn, og, out)
                 w_bf[c][:, x0:x1, :, :].rearrange("p x m r -> p (x m r)"),
             )
 
-        interleaved = {}
+        def prepx(eng, c, u0, r0, r1):
+            for r in range(r0, r1):
+                dst, src, scale = mt[(c, u0)][:, r, :], m_raw[(c, u0)][:, r, :], t_sb[:, c, r : r + 1]
+                if eng == "S":
+                    nc.scalar.activation(out=dst, in_=src, func=ACT.Copy, scale=scale)
+                elif eng == "V":
+                    nc.vector.tensor_scalar(out=dst, in0=src, scalar1=scale, scalar2=None, op0=ALU.mult)
+                else:
+                    nc.gpsimd.tensor_scalar(out=dst, in0=src, scalar1=scale, scalar2=0.0, op0=ALU.mult, op1=ALU.add)
 
-        def prep(eng, c, u, m0=0, m1=QT):
-            u0 = max(g[1] for g in m_groups if g[0] == c and g[1] <= u)
-            src = m_raw[(c, u0)][:, :, (u - u0) * QT + m0 : (u - u0) * QT + m1]
-            if eng == "S":
-                interleaved[(c, u)] = False
-                dst = mt[c][u][:].rearrange("p (r m) -> p r m", r=PACK)
-                for r in range(PACK):
-                    nc.scalar.activation(out=dst[:, r, m0:m1], in_=src[:, r, :], func=ACT.Copy, scale=t_sb[:, c, r : r + 1])
-            else:
-                interleaved[(c, u)] = True
-                dst = mt[c][u][:].rearrange("p (m r) -> p m r", r=PACK)[:, m0:m1, :]
-                e = nc.vector if eng == "V" else nc.gpsimd
-                e.tensor_tensor(
-                    out=dst,
-                    in0=src.rearrange("p r m -> p m r"),
-                    in1=t_sb[:, c, :].unsqueeze(1).to_broadcast([P, m1 - m0, PACK]),
-                    op=ALU.mult,
-                )
+        def load_gn():
+            nc.sync.dma_start(out=gn_sb[:], in_=gn)
+
+        def table():
+            nc.scalar.activation(out=warm2[:], in_=warm[:], func=ACT.Abs_reciprocal_sqrt)
+
+        def rsq(u, h0, h1):
+            nc.scalar.activation(
+                out=rstd[u][:, h0:h1], in_=ssq[u][:, h0:h1], func=ACT.Abs_reciprocal_sqrt, scale=1.0 / E, bias=256.0 * 1e-5
+            )
 
         def scores(c, u):
             b = (c * TILES + u) % SCORE_BANKS
@@ -196,10 +196,8 @@ def tile_rows_a_relu_mask_onorm_gate_kernel(tc, qT, kT, t, v, mask, gn, og, out)
 
         def weigh(c, u, h):
             b = (c * TILES + u) % SCORE_BANKS
-            if interleaved[(c, u)]:
-                f = mt[c][u][:].rearrange("p (m r) -> p m r", r=PACK)
-            else:
-                f = mt[c][u][:].rearrange("p (r m) -> p m r", r=PACK)
+            u0 = max(g[1] for g in m_groups if g[0] == c and g[1] <= u)
+            f = mt[(c, u0)][:, :, (u - u0) * QT : (u - u0 + 1) * QT].rearrange("p r m -> p m r")
             nc.vector.scalar_tensor_tensor(
                 out=w_bf[c][:, u * H + h, :, :],
                 in0=score[h][b][:].rearrange("p r m -> p m r"),
@@ -237,13 +235,7 @@ def tile_rows_a_relu_mask_onorm_gate_kernel(tc, qT, kT, t, v, mask, gn, og, out)
             )
 
         def square(u, h):
-            nc.scalar.activation(out=squares[:], in_=y_of(u, h), func=ACT.Square, accum_out=ssq[u][:, h : h + 1])
-
-        def norm(u, h0, h1):
-            nc.gpsimd.tensor_scalar(
-                out=msq[u][:, h0:h1], in0=ssq[u][:, h0:h1], scalar1=1.0 / E, scalar2=256.0 * 1e-5, op0=ALU.mult, op1=ALU.add
-            )
-            nc.gpsimd.tensor_tensor(out=rstd[u][:, h0:h1], in0=msq[u][:, h0:h1], in1=minus_half[:, h0:h1], op=ALU.pow)
+            nc.scalar.activation(out=squares[:, u * H + h, :], in_=y_of(u, h), func=ACT.Square, accum_out=ssq[u][:, h : h + 1])
 
         def finish(u, h):
             nc.vector.scalar_tensor_tensor(
@@ -263,64 +255,60 @@ def tile_rows_a_relu_mask_onorm_gate_kernel(tc, qT, kT, t, v, mask, gn, og, out)
 
         ctx.enter_context(tc.manual_schedule())
         nc.scalar.dma_start(out=t_sb[:], in_=t.rearrange("(c p r) o -> p c (r o)", c=PASSES, r=PACK))
-        nc.vector.memset(warm[:], 0.0)
+        nc.vector.memset(warm[:], 1.0)
         nc.scalar.activation(out=warm2[:], in_=warm[:], func=ACT.Sigmoid)
-        nc.gpsimd.memset(minus_half[:], -0.5)
         load_k(0, 0)
-        load_q(0)
         load_k(0, 1)
-        load_m(0, 0)
+        load_q(0)
         load_q(1)
+        load_m(0, 0)
         load_m(0, 1)
         load_q(2)
         load_m(0, 2)
         load_k(1, 0)
-        load_m(0, 3)
         load_k(1, 1)
         load_m(1, 0)
-        load_v(0)
-        load_m(1, 2)
-        load_v(1)
-        load_m(1, 3)
-        nc.sync.dma_start(out=gn_sb[:], in_=gn)
+        load_gn()
         load_og(0)
+        load_m(1, 2)
         load_og(1)
+        load_v(0)
+        load_v(1)
         pack_k("V", 0, 0, 0, 4)
-        pack_q("S", 0)
         quant_k0(0, 0)
         quant_k0(0, 1)
         quant_k0(0, 2)
         quant_k0(0, 3)
-        quant_q(0, 1)
         pack_k("V", 0, 1, 0, 2)
         pack_k("S", 0, 1, 2, 4)
         quant_k0(1, 0)
         quant_k0(1, 1)
+        pack_q("V", 0)
         quant_k0(1, 2)
         quant_k0(1, 3)
+        quant_q(0, 1)
         scores(0, 0)
-        prep("V", 0, 0)
-        pack_q("S", 1)
-        prep("G", 0, 1)
-        weigh(0, 0, 0)
+        pack_q("V", 1)
         quant_q(1, 2)
         scores(0, 1)
+        prepx("V", 0, 0, 0, 2)
+        prepx("S", 0, 0, 2, 4)
+        prepx("S", 0, 1, 0, 4)
+        weigh(0, 0, 0)
         weigh(0, 0, 1)
+        pack_q("V", 3)
         pack_q("S", 2)
-        pack_q("S", 3)
-        prep("G", 0, 2)
         weigh(0, 1, 0)
         quant_q(2, 4)
         scores(0, 2)
-        weigh(0, 1, 1)
         scores(0, 3)
-        pack_k("S", 1, 0, 0, 4)
-        prep("G", 0, 3)
-        weigh(0, 2, 0)
+        weigh(0, 1, 1)
+        prepx("S", 0, 2, 0, 4)
         quant_w(0, 0, 4)
-        weigh(0, 2, 1)
+        pack_k("S", 1, 0, 0, 4)
         pack_k("S", 1, 1, 0, 4)
-        prep("G", 1, 0)
+        weigh(0, 2, 0)
+        weigh(0, 2, 1)
         weigh(0, 3, 0)
         weigh(0, 3, 1)
         quant_k1(0, 2)
@@ -328,66 +316,64 @@ def tile_rows_a_relu_mask_onorm_gate_kernel(tc, qT, kT, t, v, mask, gn, og, out)
         scores(1, 0)
         scores(1, 1)
         quant_w(0, 4, 8)
-        prep("G", 1, 1)
-        pack_v("S", 0, 0)
-        pack_v("S", 0, 1)
+        prepx("S", 1, 0, 0, 4)
+        sigmoid(0)
+        make_gate("G", 0)
+        make_gate("G", 1)
+        prepx("S", 1, 2, 0, 4)
+        sigmoid(1)
+        make_gate("G", 2)
         weigh(1, 0, 0)
         weigh(1, 0, 1)
         scores(1, 2)
-        prep("G", 1, 2)
-        pack_v("S", 1, 0)
-        pack_v("S", 1, 1)
         weigh(1, 1, 0)
-        quant_w(1, 0, 2)
         weigh(1, 1, 1)
         scores(1, 3)
-        quant_v(0)
-        prep("G", 1, 3)
+        pack_v("S", 0, 0)
+        pack_v("S", 0, 1)
+        pack_v("S", 1, 0)
+        pack_v("S", 1, 1)
+        table()
         weigh(1, 2, 0)
-        quant_w(1, 2, 4)
+        quant_w(1, 0, 4)
+        weigh(1, 2, 1)
+        quant_v(0)
         quant_v(1)
         values(0, 0)
         values(0, 1)
         values(1, 0)
         values(1, 1)
-        weigh(1, 2, 1)
-        sigmoid(0)
+        quant_w(1, 4, 6)
+        weigh(1, 3, 0)
+        weigh(1, 3, 1)
         square(0, 0)
         square(0, 1)
-        square(1, 0)
-        square(1, 1)
-        make_gate("G", 0)
-        norm(0, 0, 2)
-        make_gate("G", 1)
-        norm(1, 0, 2)
-        sigmoid(1)
-        weigh(1, 3, 0)
-        quant_w(1, 4, 6)
         values(2, 0)
         values(2, 1)
-        weigh(1, 3, 1)
+        square(1, 0)
+        square(1, 1)
+        rsq(0, 0, 2)
         quant_w(1, 6, 7)
-        values(3, 0)
         quant_w(1, 7, 8)
+        values(3, 0)
         values(3, 1)
+        rsq(1, 0, 2)
         square(2, 0)
         square(2, 1)
+        make_gate("V", 3)
         finish(0, 0)
         finish(0, 1)
         store(0, 0, 2)
-        make_gate("G", 2)
-        norm(2, 0, 2)
-        make_gate("G", 3)
         square(3, 0)
-        norm(3, 0, 1)
+        rsq(2, 0, 2)
         square(3, 1)
-        norm(3, 1, 2)
-        finish(1, 0)
-        finish(1, 1)
-        store(1, 0, 2)
+        rsq(3, 0, 2)
         finish(2, 0)
         finish(2, 1)
         store(2, 0, 2)
+        finish(1, 0)
+        finish(1, 1)
+        store(1, 0, 2)
         finish(3, 0)
         finish(3, 1)
         store(3, 0, 2)

@@ -21,7 +21,7 @@ PASSES = N // TOK
 QT = 128
 TILES = NQ // QT
 HALF = TOK // 2
-SCORE_BANKS = 3
+SCORE_BANKS = 2
 
 
 def tile_rows_a_relu_mask_onorm_gate_kernel(tc, qT, kT, t, v, mask, gn, og, out):
@@ -34,14 +34,17 @@ def tile_rows_a_relu_mask_onorm_gate_kernel(tc, qT, kT, t, v, mask, gn, og, out)
             return sb.tile(shape, dtype, name=name, align_bytes=64)
 
         score = [[ps.tile([P, PACK, QT], F32, name="score%d_%d" % (h, b)) for b in range(SCORE_BANKS)] for h in range(H)]
-        y = [ps.tile([P, 4, E], F32, name="y%d" % b) for b in range(2)]
+        y = [ps.tile([P, H, E], F32, name="y%d" % u) for u in range(TILES)]
 
         t_sb = sbuf("t_sb", [P, PASSES, PACK], F32)
         gn_sb = sbuf("gn_sb", [P, E], F32)
-        q_groups = [(0, 1), (1, 1), (2, 2)]
+        q_groups = [(0, 2), (2, 2)]
         q_raw = {u0: sbuf("q_raw%d" % u0, [P, PACK, n * QT], F32) for u0, n in q_groups}
-        k_raw = [[sbuf("k_raw%d_%d" % (c, a), [P, PACK, HALF], F32) for a in range(2)] for c in range(PASSES)]
-        m_groups = [(0, 0, 1), (0, 1, 1), (0, 2, 2), (1, 0, 2), (1, 2, 2)]
+        k_raw = [[sbuf("k_raw0_%d" % a, [P, PACK, HALF], F32) for a in range(2)]]
+        k1_raw = sbuf("k1_raw", [P, PACK, TOK], F32)
+        k_raw.append([k1_raw[:, :, :HALF], k1_raw[:, :, HALF:]])
+        mi = [[sbuf("mi%d_%d" % (c, u), [P, QT, PACK], F32) for u in range(TILES)] for c in range(PASSES)]
+        m_groups = [(0, 0, 2), (0, 2, 2), (1, 0, 2), (1, 2, 2)]
         m_raw = {(c, u0): sbuf("m_raw%d_%d" % (c, u0), [P, PACK, n * QT], F32) for c, u0, n in m_groups}
         v_raw = [sbuf("v_raw%d" % h, [P, PASSES, PACK, E], F32) for h in range(H)]
         og_sb = [sbuf("og_sb%d" % a, [P, H, 2, E], F32) for a in range(2)]
@@ -107,18 +110,18 @@ def tile_rows_a_relu_mask_onorm_gate_kernel(tc, qT, kT, t, v, mask, gn, og, out)
                 nc.gpsimd.tensor_scalar(out=dst, in0=src, scalar1=1.0, scalar2=0.0, op0=ALU.mult, op1=ALU.add)
 
         def pack_q(eng, u):
-            u0 = min(u, 2)
+            u0 = u - u % 2
             src = q_raw[u0][:, :, (u - u0) * QT : (u - u0 + 1) * QT]
             dst = q_bf[:, u * QT : (u + 1) * QT, :]
             cast(eng, dst.rearrange("p (g i) j -> p g j i", i=4), src.rearrange("p j (g i) -> p g j i", i=4))
 
         def pack_k(eng, c, a, r0, r1):
-            src = k_raw[c][a][:].rearrange("p j (s r) -> p s r j", r=PACK)[:, :, r0:r1, :]
+            src = k_raw[c][a][:].rearrange("p j (s r) -> p s j r", r=PACK)[:, :, :, r0:r1]
             if c == 0:
                 dst = k0_bf[a][:, r0:r1, :, :]
             else:
                 dst = k1_bf[:, r0:r1, a * 64 : (a + 1) * 64, :]
-            cast(eng, dst.rearrange("p r s j -> p s r j"), src)
+            cast(eng, dst.rearrange("p r s j -> p s j r"), src)
 
         def pack_v(eng, h, c):
             src = v_raw[h][:, c, :, :]
@@ -167,6 +170,17 @@ def tile_rows_a_relu_mask_onorm_gate_kernel(tc, qT, kT, t, v, mask, gn, og, out)
                 else:
                     nc.gpsimd.tensor_scalar(out=dst, in0=src, scalar1=scale, scalar2=0.0, op0=ALU.mult, op1=ALU.add)
 
+        def load_kk(c):
+            nc.sync.dma_start(out=k1_raw[:], in_=k_hbm[:, :, TOK:])
+
+        def prept(eng, c, u0, r):
+            prepx(eng, c, u0, r, r + 1)
+
+        def il(eng, c, u):
+            u0 = u - u % 2
+            src = mt[(c, u0)][:, :, (u - u0) * QT : (u - u0 + 1) * QT]
+            cast(eng, mi[c][u][:].rearrange("p (g i) r -> p g r i", i=4), src.rearrange("p r (g i) -> p g r i", i=4))
+
         def load_gn():
             nc.sync.dma_start(out=gn_sb[:], in_=gn)
 
@@ -180,8 +194,8 @@ def tile_rows_a_relu_mask_onorm_gate_kernel(tc, qT, kT, t, v, mask, gn, og, out)
 
         def scores(c, u):
             b = (c * TILES + u) % SCORE_BANKS
-            for r in range(PACK):
-                for h in range(H):
+            for h in range(H):
+                for r in range(PACK):
                     rows = slice(h * ROWS, (h + 1) * ROWS)
                     cols = slice(u * QT, (u + 1) * QT)
                     nc.tensor.matmul_mx(
@@ -196,8 +210,7 @@ def tile_rows_a_relu_mask_onorm_gate_kernel(tc, qT, kT, t, v, mask, gn, og, out)
 
         def weigh(c, u, h):
             b = (c * TILES + u) % SCORE_BANKS
-            u0 = max(g[1] for g in m_groups if g[0] == c and g[1] <= u)
-            f = mt[(c, u0)][:, :, (u - u0) * QT : (u - u0 + 1) * QT].rearrange("p r m -> p m r")
+            f = mi[c][u][:]
             nc.vector.scalar_tensor_tensor(
                 out=w_bf[c][:, u * H + h, :, :],
                 in0=score[h][b][:].rearrange("p r m -> p m r"),
@@ -208,7 +221,7 @@ def tile_rows_a_relu_mask_onorm_gate_kernel(tc, qT, kT, t, v, mask, gn, og, out)
             )
 
         def y_of(u, h):
-            return y[u % 2][:, (u // 2) * H + h, :]
+            return y[u][:, h, :]
 
         def values(u, h):
             for c in range(PASSES):
@@ -260,20 +273,17 @@ def tile_rows_a_relu_mask_onorm_gate_kernel(tc, qT, kT, t, v, mask, gn, og, out)
         load_k(0, 0)
         load_k(0, 1)
         load_q(0)
-        load_q(1)
         load_m(0, 0)
-        load_m(0, 1)
         load_q(2)
         load_m(0, 2)
-        load_k(1, 0)
-        load_k(1, 1)
+        load_kk(1)
         load_m(1, 0)
+        load_m(1, 2)
         load_gn()
         load_og(0)
-        load_m(1, 2)
-        load_og(1)
         load_v(0)
         load_v(1)
+        load_og(1)
         pack_k("V", 0, 0, 0, 4)
         quant_k0(0, 0)
         quant_k0(0, 1)
@@ -283,46 +293,62 @@ def tile_rows_a_relu_mask_onorm_gate_kernel(tc, qT, kT, t, v, mask, gn, og, out)
         pack_k("S", 0, 1, 2, 4)
         quant_k0(1, 0)
         quant_k0(1, 1)
-        pack_q("V", 0)
         quant_k0(1, 2)
         quant_k0(1, 3)
+        pack_q("V", 0)
+        pack_q("S", 1)
         quant_q(0, 1)
-        scores(0, 0)
-        pack_q("V", 1)
         quant_q(1, 2)
+        scores(0, 0)
         scores(0, 1)
-        prepx("V", 0, 0, 0, 2)
-        prepx("S", 0, 0, 2, 4)
-        prepx("S", 0, 1, 0, 4)
+        prept("V", 0, 0, 0)
+        prept("V", 0, 0, 1)
+        prept("V", 0, 0, 2)
+        prept("S", 0, 0, 3)
+        il("V", 0, 0)
+        il("S", 0, 1)
+        pack_q("S", 2)
+        pack_q("S", 3)
         weigh(0, 0, 0)
         weigh(0, 0, 1)
-        pack_q("V", 3)
-        pack_q("S", 2)
         weigh(0, 1, 0)
         quant_q(2, 4)
         scores(0, 2)
-        scores(0, 3)
         weigh(0, 1, 1)
-        prepx("S", 0, 2, 0, 4)
+        scores(0, 3)
+        prept("S", 0, 2, 0)
+        prept("S", 0, 2, 1)
+        prept("S", 0, 2, 2)
+        prept("S", 0, 2, 3)
         quant_w(0, 0, 4)
-        pack_k("S", 1, 0, 0, 4)
-        pack_k("S", 1, 1, 0, 4)
+        il("V", 0, 2)
+        il("V", 0, 3)
+        pack_k("V", 1, 0, 0, 2)
+        pack_k("S", 1, 1, 0, 2)
+        pack_k("S", 1, 0, 2, 4)
+        pack_k("S", 1, 1, 2, 4)
         weigh(0, 2, 0)
         weigh(0, 2, 1)
         weigh(0, 3, 0)
-        weigh(0, 3, 1)
         quant_k1(0, 2)
+        weigh(0, 3, 1)
         quant_k1(2, 4)
         scores(1, 0)
         scores(1, 1)
+        prept("S", 1, 0, 0)
+        prept("S", 1, 0, 1)
+        prept("S", 1, 0, 2)
+        prept("S", 1, 0, 3)
+        prept("V", 1, 2, 0)
+        prept("V", 1, 2, 1)
         quant_w(0, 4, 8)
-        prepx("S", 1, 0, 0, 4)
+        il("V", 1, 0)
+        il("V", 1, 1)
+        prept("S", 1, 2, 2)
+        prept("S", 1, 2, 3)
         sigmoid(0)
         make_gate("G", 0)
         make_gate("G", 1)
-        prepx("S", 1, 2, 0, 4)
-        sigmoid(1)
-        make_gate("G", 2)
         weigh(1, 0, 0)
         weigh(1, 0, 1)
         scores(1, 2)
@@ -331,49 +357,53 @@ def tile_rows_a_relu_mask_onorm_gate_kernel(tc, qT, kT, t, v, mask, gn, og, out)
         scores(1, 3)
         pack_v("S", 0, 0)
         pack_v("S", 0, 1)
+        il("S", 1, 3)
         pack_v("S", 1, 0)
         pack_v("S", 1, 1)
+        sigmoid(1)
         table()
-        weigh(1, 2, 0)
+        il("V", 1, 2)
         quant_w(1, 0, 4)
-        weigh(1, 2, 1)
         quant_v(0)
-        quant_v(1)
         values(0, 0)
-        values(0, 1)
         values(1, 0)
+        weigh(1, 2, 0)
+        weigh(1, 2, 1)
+        quant_v(1)
+        values(0, 1)
         values(1, 1)
-        quant_w(1, 4, 6)
         weigh(1, 3, 0)
-        weigh(1, 3, 1)
-        square(0, 0)
-        square(0, 1)
+        quant_w(1, 4, 6)
         values(2, 0)
         values(2, 1)
-        square(1, 0)
-        square(1, 1)
-        rsq(0, 0, 2)
+        weigh(1, 3, 1)
         quant_w(1, 6, 7)
         quant_w(1, 7, 8)
+        square(0, 0)
+        square(0, 1)
+        square(1, 0)
+        square(1, 1)
         values(3, 0)
         values(3, 1)
+        rsq(0, 0, 2)
         rsq(1, 0, 2)
         square(2, 0)
         square(2, 1)
+        square(3, 0)
+        square(3, 1)
+        rsq(2, 0, 2)
+        rsq(3, 0, 2)
+        make_gate("V", 2)
         make_gate("V", 3)
         finish(0, 0)
         finish(0, 1)
         store(0, 0, 2)
-        square(3, 0)
-        rsq(2, 0, 2)
-        square(3, 1)
-        rsq(3, 0, 2)
-        finish(2, 0)
-        finish(2, 1)
-        store(2, 0, 2)
         finish(1, 0)
         finish(1, 1)
         store(1, 0, 2)
+        finish(2, 0)
+        finish(2, 1)
+        store(2, 0, 2)
         finish(3, 0)
         finish(3, 1)
         store(3, 0, 2)

@@ -179,7 +179,10 @@ def tile_rows_a_relu_mask_onorm_gate_kernel(tc, qT, kT, t, v, mask, gn, og, out)
         def il(eng, c, u):
             u0 = u - u % 2
             src = mt[(c, u0)][:, :, (u - u0) * QT : (u - u0 + 1) * QT]
-            cast(eng, mi[c][u][:].rearrange("p (g i) r -> p g r i", i=4), src.rearrange("p r (g i) -> p g r i", i=4))
+            if eng == "G":
+                cast(eng, mi[c][u][:], src.rearrange("p r m -> p m r"))
+            else:
+                cast(eng, mi[c][u][:].rearrange("p (g i) r -> p g r i", i=4), src.rearrange("p r (g i) -> p g r i", i=4))
 
         def load_gn():
             nc.sync.dma_start(out=gn_sb[:], in_=gn)
@@ -274,14 +277,14 @@ def tile_rows_a_relu_mask_onorm_gate_kernel(tc, qT, kT, t, v, mask, gn, og, out)
         load_k(0, 1)
         load_q(0)
         load_m(0, 0)
-        load_q(2)
         load_m(0, 2)
+        load_q(2)
         load_kk(1)
         load_m(1, 0)
-        load_m(1, 2)
         load_gn()
-        load_og(0)
+        load_m(1, 2)
         load_v(0)
+        load_og(0)
         load_v(1)
         load_og(1)
         pack_k("V", 0, 0, 0, 4)
@@ -303,75 +306,75 @@ def tile_rows_a_relu_mask_onorm_gate_kernel(tc, qT, kT, t, v, mask, gn, og, out)
         scores(0, 1)
         prept("V", 0, 0, 0)
         prept("V", 0, 0, 1)
-        prept("V", 0, 0, 2)
+        prept("S", 0, 0, 2)
         prept("S", 0, 0, 3)
         il("V", 0, 0)
         il("S", 0, 1)
-        pack_q("S", 2)
-        pack_q("S", 3)
+        prept("G", 0, 2, 0)
+        prept("G", 0, 2, 1)
+        prept("S", 0, 2, 2)
+        prept("S", 0, 2, 3)
         weigh(0, 0, 0)
         weigh(0, 0, 1)
         weigh(0, 1, 0)
+        weigh(0, 1, 1)
+        pack_q("S", 2)
+        pack_q("S", 3)
+        il("S", 0, 2)
+        il("V", 0, 3)
         quant_q(2, 4)
         scores(0, 2)
-        weigh(0, 1, 1)
         scores(0, 3)
-        prept("S", 0, 2, 0)
-        prept("S", 0, 2, 1)
-        prept("S", 0, 2, 2)
-        prept("S", 0, 2, 3)
         quant_w(0, 0, 4)
-        il("V", 0, 2)
-        il("V", 0, 3)
         pack_k("V", 1, 0, 0, 2)
         pack_k("S", 1, 1, 0, 2)
         pack_k("S", 1, 0, 2, 4)
         pack_k("S", 1, 1, 2, 4)
         weigh(0, 2, 0)
+        quant_k1(0, 2)
+        prept("G", 1, 0, 0)
+        prept("G", 1, 0, 1)
+        prept("S", 1, 0, 2)
+        prept("S", 1, 0, 3)
         weigh(0, 2, 1)
         weigh(0, 3, 0)
-        quant_k1(0, 2)
         weigh(0, 3, 1)
         quant_k1(2, 4)
         scores(1, 0)
         scores(1, 1)
-        prept("S", 1, 0, 0)
-        prept("S", 1, 0, 1)
-        prept("S", 1, 0, 2)
-        prept("S", 1, 0, 3)
         prept("V", 1, 2, 0)
-        prept("V", 1, 2, 1)
         quant_w(0, 4, 8)
-        il("V", 1, 0)
-        il("V", 1, 1)
-        prept("S", 1, 2, 2)
+        prept("V", 1, 2, 1)
         prept("S", 1, 2, 3)
-        sigmoid(0)
-        make_gate("G", 0)
-        make_gate("G", 1)
+        il("S", 1, 0)
+        il("G", 1, 1)
         weigh(1, 0, 0)
         weigh(1, 0, 1)
         scores(1, 2)
+        prept("V", 1, 2, 2)
+        pack_v("S", 0, 0)
+        sigmoid(0)
+        make_gate("G", 0)
+        pack_v("S", 0, 1)
         weigh(1, 1, 0)
         weigh(1, 1, 1)
         scores(1, 3)
-        pack_v("S", 0, 0)
-        pack_v("S", 0, 1)
-        il("S", 1, 3)
         pack_v("S", 1, 0)
         pack_v("S", 1, 1)
         sigmoid(1)
+        il("S", 1, 3)
         table()
         il("V", 1, 2)
         quant_w(1, 0, 4)
         quant_v(0)
+        quant_v(1)
+        make_gate("G", 1)
         values(0, 0)
+        values(0, 1)
         values(1, 0)
+        values(1, 1)
         weigh(1, 2, 0)
         weigh(1, 2, 1)
-        quant_v(1)
-        values(0, 1)
-        values(1, 1)
         weigh(1, 3, 0)
         quant_w(1, 4, 6)
         values(2, 0)
@@ -379,25 +382,25 @@ def tile_rows_a_relu_mask_onorm_gate_kernel(tc, qT, kT, t, v, mask, gn, og, out)
         weigh(1, 3, 1)
         quant_w(1, 6, 7)
         quant_w(1, 7, 8)
+        values(3, 0)
+        values(3, 1)
         square(0, 0)
         square(0, 1)
         square(1, 0)
-        square(1, 1)
-        values(3, 0)
-        values(3, 1)
         rsq(0, 0, 2)
-        rsq(1, 0, 2)
+        square(1, 1)
         square(2, 0)
+        rsq(1, 0, 2)
         square(2, 1)
         square(3, 0)
-        square(3, 1)
         rsq(2, 0, 2)
+        square(3, 1)
         rsq(3, 0, 2)
         make_gate("V", 2)
-        make_gate("V", 3)
         finish(0, 0)
         finish(0, 1)
         store(0, 0, 2)
+        make_gate("V", 3)
         finish(1, 0)
         finish(1, 1)
         store(1, 0, 2)
@@ -405,5 +408,6 @@ def tile_rows_a_relu_mask_onorm_gate_kernel(tc, qT, kT, t, v, mask, gn, og, out)
         finish(2, 1)
         store(2, 0, 2)
         finish(3, 0)
+        store(3, 0, 1)
         finish(3, 1)
-        store(3, 0, 2)
+        store(3, 1, 2)

from contextlib import ExitStack

import concourse.mybir as mybir

H, D, NQ, N, E = 2, 256, 512, 1024, 128
FLOPS = 2 * H * N * NQ * (D + E)

F32 = mybir.dt.float32
BF16 = mybir.dt.bfloat16
U32 = mybir.dt.uint32
U8 = mybir.dt.uint8
FP8X4 = mybir.dt.float8_e4m3fn_x4
ALU = mybir.AluOpType
ACT = mybir.ActivationFunctionType

P = 128
PACK = 4
ROWS = D // PACK
TOK = P * PACK
PASSES = N // TOK
QT = 128
TILES = NQ // QT
HALF = TOK // 2
SCORE_BANKS = 2


def tile_rows_a_relu_mask_onorm_gate_kernel(tc, qT, kT, t, v, mask, gn, og, out):
    nc = tc.nc
    with ExitStack() as ctx:
        sb = ctx.enter_context(tc.tile_pool(name="sb", bufs=1))
        ps = ctx.enter_context(tc.psum_pool(name="ps", bufs=1))

        def sbuf(name, shape, dtype):
            return sb.tile(shape, dtype, name=name, align_bytes=64)

        score = [[ps.tile([P, PACK, QT], F32, name="score%d_%d" % (h, b)) for b in range(SCORE_BANKS)] for h in range(H)]
        y = [ps.tile([P, H, E], F32, name="y%d" % u) for u in range(TILES)]

        t_sb = sbuf("t_sb", [P, PASSES, PACK], F32)
        gn_sb = sbuf("gn_sb", [P, E], F32)
        q_groups = [(0, 2), (2, 2)]
        q_raw = {u0: sbuf("q_raw%d" % u0, [P, PACK, n * QT], F32) for u0, n in q_groups}
        k_raw = [[sbuf("k_raw0_%d" % a, [P, PACK, HALF], F32) for a in range(2)]]
        k1_raw = sbuf("k1_raw", [P, PACK, TOK], F32)
        k_raw.append([k1_raw[:, :, :HALF], k1_raw[:, :, HALF:]])
        mi = [[sbuf("mi%d_%d" % (c, u), [P, QT, PACK], F32) for u in range(TILES)] for c in range(PASSES)]
        m_groups = [(0, 0, 2), (0, 2, 2), (1, 0, 2), (1, 2, 2)]
        m_raw = {(c, u0): sbuf("m_raw%d_%d" % (c, u0), [P, PACK, n * QT], F32) for c, u0, n in m_groups}
        v_raw = [sbuf("v_raw%d" % h, [P, PASSES, PACK, E], F32) for h in range(H)]
        og_sb = [sbuf("og_sb%d" % a, [P, H, 2, E], F32) for a in range(2)]

        q_bf = sbuf("q_bf", [P, NQ, PACK], BF16)
        q_codes = sbuf("q_codes", [P, NQ], U32)
        q_scales = sbuf("q_scales", [P, NQ], U8)
        k0_bf = [sbuf("k0_bf%d" % a, [P, PACK, P // 2, PACK], BF16) for a in range(2)]
        k1_bf = sbuf("k1_bf", [P, PACK, P, PACK], BF16)
        k_codes = [sbuf("k_codes%d" % c, [P, PACK, P], U32) for c in range(PASSES)]
        k_scales = [sbuf("k_scales%d" % c, [P, PACK, P], U8) for c in range(PASSES)]
        v_bf = [sbuf("v_bf%d" % h, [P, PASSES, E, PACK], BF16) for h in range(H)]
        v_codes = [sbuf("v_codes%d" % h, [P, PASSES, E], U32) for h in range(H)]
        v_scales = [sbuf("v_scales%d" % h, [P, PASSES, E], U8) for h in range(H)]
        mt = {(c, u0): sbuf("mt%d_%d" % (c, u0), [P, PACK, n * QT], F32) for c, u0, n in m_groups}
        w_bf = [sbuf("w_bf%d" % c, [P, TILES * H, QT, PACK], BF16) for c in range(PASSES)]
        w_codes = [sbuf("w_codes%d" % c, [P, TILES * H, QT], U32) for c in range(PASSES)]
        w_scales = [sbuf("w_scales%d" % c, [P, TILES * H, QT], U8) for c in range(PASSES)]
        sig = [sbuf("sig%d" % a, [P, H, 2, E], F32) for a in range(2)]
        gate = [sbuf("gate%d" % u, [P, H, E], F32) for u in range(TILES)]
        squares = sbuf("squares", [P, TILES * H, E], BF16)
        ssq = [sbuf("ssq%d" % u, [P, H], F32) for u in range(TILES)]
        rstd = [sbuf("rstd%d" % u, [P, H], F32) for u in range(TILES)]
        res = [sbuf("res%d" % u, [P, H, E], F32) for u in range(TILES)]
        warm = sbuf("warm", [P, 8], F32)
        warm2 = sbuf("warm2", [P, 8], F32)

        q_hbm = qT.rearrange("h (p j) q -> (h p) j q", j=PACK)
        k_hbm = kT.rearrange("h (p j) i -> (h p) j i", j=PACK)
        m_hbm = mask.rearrange("(c p r) q -> c p r q", c=PASSES, r=PACK)

        def load_q(u0):
            n = q_raw[u0].shape[2]
            nc.sync.dma_start(out=q_raw[u0][:], in_=q_hbm[:, :, u0 * QT : u0 * QT + n])

        def load_k(c, a):
            i0 = c * TOK + a * HALF
            nc.sync.dma_start(out=k_raw[c][a][:], in_=k_hbm[:, :, i0 : i0 + HALF])

        def load_m(c, u0):
            n = m_raw[(c, u0)].shape[2]
            nc.sync.dma_start(out=m_raw[(c, u0)][:], in_=m_hbm[c][:, :, u0 * QT : u0 * QT + n])

        def load_v(h):
            nc.sync.dma_start(
                out=v_raw[h][:].rearrange("p c r e -> p c (r e)"),
                in_=v[h].rearrange("(c p r) e -> p c (r e)", c=PASSES, r=PACK),
            )

        def load_og(a):
            for h in range(H):
                nc.sync.dma_start(
                    out=og_sb[a][:, h, :, :],
                    in_=og[h][a * 2 * QT : (a + 1) * 2 * QT, :].rearrange("(u p) e -> p u e", p=P),
                )

        def cast(eng, dst, src):
            if eng == "V":
                nc.vector.tensor_copy(out=dst, in_=src)
            elif eng == "S":
                nc.scalar.copy(out=dst, in_=src)
            else:
                nc.gpsimd.tensor_scalar(out=dst, in0=src, scalar1=1.0, scalar2=0.0, op0=ALU.mult, op1=ALU.add)

        def pack_q(eng, u):
            u0 = u - u % 2
            src = q_raw[u0][:, :, (u - u0) * QT : (u - u0 + 1) * QT]
            dst = q_bf[:, u * QT : (u + 1) * QT, :]
            cast(eng, dst.rearrange("p (g i) j -> p g j i", i=4), src.rearrange("p j (g i) -> p g j i", i=4))

        def pack_k(eng, c, a, r0, r1):
            src = k_raw[c][a][:].rearrange("p j (s r) -> p s j r", r=PACK)[:, :, :, r0:r1]
            if c == 0:
                dst = k0_bf[a][:, r0:r1, :, :]
            else:
                dst = k1_bf[:, r0:r1, a * 64 : (a + 1) * 64, :]
            cast(eng, dst.rearrange("p r s j -> p s j r"), src)

        def pack_v(eng, h, c):
            src = v_raw[h][:, c, :, :]
            dst = v_bf[h][:, c, :, :]
            cast(eng, dst.rearrange("p (g i) r -> p g r i", i=4), src.rearrange("p r (g i) -> p g r i", i=4))

        def quant(codes, scales, src):
            nc.vector.quantize_mx(out=codes.bitcast(FP8X4), scales=scales, in_=src)

        def quant_q(u0, u1):
            cols = slice(u0 * QT, u1 * QT)
            quant(q_codes[:, cols], q_scales[:, cols], q_bf[:, cols, :].rearrange("p q j -> p (q j)"))

        def quant_k0(a, r):
            cols = slice(a * 64, (a + 1) * 64)
            quant(k_codes[0][:, r, cols], k_scales[0][:, r, cols], k0_bf[a][:, r, :, :].rearrange("p s j -> p (s j)"))

        def quant_k1(r0, r1):
            quant(
                k_codes[1][:, r0:r1, :].rearrange("p r s -> p (r s)"),
                k_scales[1][:, r0:r1, :].rearrange("p r s -> p (r s)"),
                k1_bf[:, r0:r1, :, :].rearrange("p r s j -> p (r s j)"),
            )

        def quant_v(h):
            quant(
                v_codes[h][:].rearrange("p c e -> p (c e)"),
                v_scales[h][:].rearrange("p c e -> p (c e)"),
                v_bf[h][:].rearrange("p c e r -> p (c e r)"),
            )

        def quant_w(c, x0, x1):
            quant(
                w_codes[c][:, x0:x1, :].rearrange("p x m -> p (x m)"),
                w_scales[c][:, x0:x1, :].rearrange("p x m -> p (x m)"),
                w_bf[c][:, x0:x1, :, :].rearrange("p x m r -> p (x m r)"),
            )

        def prepx(eng, c, u0, r0, r1):
            for r in range(r0, r1):
                dst, src, scale = mt[(c, u0)][:, r, :], m_raw[(c, u0)][:, r, :], t_sb[:, c, r : r + 1]
                if eng == "S":
                    nc.scalar.activation(out=dst, in_=src, func=ACT.Copy, scale=scale)
                elif eng == "V":
                    nc.vector.tensor_scalar(out=dst, in0=src, scalar1=scale, scalar2=None, op0=ALU.mult)
                else:
                    nc.gpsimd.tensor_scalar(out=dst, in0=src, scalar1=scale, scalar2=0.0, op0=ALU.mult, op1=ALU.add)

        def load_kk(c):
            nc.sync.dma_start(out=k1_raw[:], in_=k_hbm[:, :, TOK:])

        def prept(eng, c, u0, r):
            prepx(eng, c, u0, r, r + 1)

        def il(eng, c, u):
            u0 = u - u % 2
            src = mt[(c, u0)][:, :, (u - u0) * QT : (u - u0 + 1) * QT]
            if eng == "G":
                cast(eng, mi[c][u][:], src.rearrange("p r m -> p m r"))
            else:
                cast(eng, mi[c][u][:].rearrange("p (g i) r -> p g r i", i=4), src.rearrange("p r (g i) -> p g r i", i=4))

        def load_gn():
            nc.sync.dma_start(out=gn_sb[:], in_=gn)

        def table():
            nc.scalar.activation(out=warm2[:], in_=warm[:], func=ACT.Abs_reciprocal_sqrt)

        def rsq(u, h0, h1):
            nc.scalar.activation(
                out=rstd[u][:, h0:h1], in_=ssq[u][:, h0:h1], func=ACT.Abs_reciprocal_sqrt, scale=1.0 / E, bias=256.0 * 1e-5
            )

        def scores(c, u):
            b = (c * TILES + u) % SCORE_BANKS
            for h in range(H):
                for r in range(PACK):
                    rows = slice(h * ROWS, (h + 1) * ROWS)
                    cols = slice(u * QT, (u + 1) * QT)
                    nc.tensor.matmul_mx(
                        out=score[h][b][:, r, :],
                        lhsT=k_codes[c][rows, r, :].bitcast(FP8X4),
                        lhsT_scale=k_scales[c][rows, r, :],
                        rhs=q_codes[rows, cols].bitcast(FP8X4),
                        rhs_scale=q_scales[rows, cols],
                        start=True,
                        stop=True,
                    )

        def weigh(c, u, h):
            b = (c * TILES + u) % SCORE_BANKS
            f = mi[c][u][:]
            nc.vector.scalar_tensor_tensor(
                out=w_bf[c][:, u * H + h, :, :],
                in0=score[h][b][:].rearrange("p r m -> p m r"),
                scalar=0.0,
                in1=f,
                op0=ALU.max,
                op1=ALU.mult,
            )

        def y_of(u, h):
            return y[u][:, h, :]

        def values(u, h):
            for c in range(PASSES):
                nc.tensor.matmul_mx(
                    out=y_of(u, h),
                    lhsT=w_codes[c][:, u * H + h, :].bitcast(FP8X4),
                    lhsT_scale=w_scales[c][:, u * H + h, :],
                    rhs=v_codes[h][:, c, :].bitcast(FP8X4),
                    rhs_scale=v_scales[h][:, c, :],
                    start=(c == 0),
                    stop=(c == PASSES - 1),
                )

        def sigmoid(a):
            nc.scalar.activation(out=sig[a][:], in_=og_sb[a][:], func=ACT.Sigmoid)

        def make_gate(eng, u):
            e = nc.vector if eng == "V" else nc.gpsimd
            e.tensor_tensor(
                out=gate[u][:],
                in0=sig[u // 2][:, :, u % 2, :],
                in1=gn_sb[:].unsqueeze(1).to_broadcast([P, H, E]),
                op=ALU.mult,
            )

        def square(u, h):
            nc.scalar.activation(out=squares[:, u * H + h, :], in_=y_of(u, h), func=ACT.Square, accum_out=ssq[u][:, h : h + 1])

        def finish(u, h):
            nc.vector.scalar_tensor_tensor(
                out=res[u][:, h, :],
                in0=y_of(u, h),
                scalar=rstd[u][:, h : h + 1],
                in1=gate[u][:, h, :],
                op0=ALU.mult,
                op1=ALU.mult,
            )

        def store(u, h0, h1):
            nc.sync.dma_start(
                out=out[h0:h1, u * QT : (u + 1) * QT, :].rearrange("h p e -> p h e"),
                in_=res[u][:, h0:h1, :],
            )

        ctx.enter_context(tc.manual_schedule())
        nc.scalar.dma_start(out=t_sb[:], in_=t.rearrange("(c p r) o -> p c (r o)", c=PASSES, r=PACK))
        nc.vector.memset(warm[:], 1.0)
        nc.scalar.activation(out=warm2[:], in_=warm[:], func=ACT.Sigmoid)
        load_k(0, 0)
        load_k(0, 1)
        load_q(0)
        load_m(0, 0)
        load_m(0, 2)
        load_q(2)
        load_kk(1)
        load_m(1, 0)
        load_gn()
        load_m(1, 2)
        load_v(0)
        load_og(0)
        load_v(1)
        load_og(1)
        pack_k("V", 0, 0, 0, 4)
        quant_k0(0, 0)
        quant_k0(0, 1)
        quant_k0(0, 2)
        quant_k0(0, 3)
        pack_k("V", 0, 1, 0, 2)
        pack_k("S", 0, 1, 2, 4)
        quant_k0(1, 0)
        quant_k0(1, 1)
        quant_k0(1, 2)
        quant_k0(1, 3)
        pack_q("V", 0)
        pack_q("S", 1)
        quant_q(0, 1)
        quant_q(1, 2)
        scores(0, 0)
        scores(0, 1)
        prept("V", 0, 0, 0)
        prept("V", 0, 0, 1)
        prept("S", 0, 0, 2)
        prept("S", 0, 0, 3)
        il("V", 0, 0)
        il("S", 0, 1)
        prept("G", 0, 2, 0)
        prept("G", 0, 2, 1)
        prept("S", 0, 2, 2)
        prept("S", 0, 2, 3)
        weigh(0, 0, 0)
        weigh(0, 0, 1)
        weigh(0, 1, 0)
        weigh(0, 1, 1)
        pack_q("S", 2)
        pack_q("S", 3)
        il("S", 0, 2)
        il("V", 0, 3)
        quant_q(2, 4)
        scores(0, 2)
        scores(0, 3)
        quant_w(0, 0, 4)
        pack_k("V", 1, 0, 0, 2)
        pack_k("S", 1, 1, 0, 2)
        pack_k("S", 1, 0, 2, 4)
        pack_k("S", 1, 1, 2, 4)
        weigh(0, 2, 0)
        quant_k1(0, 2)
        prept("G", 1, 0, 0)
        prept("G", 1, 0, 1)
        prept("S", 1, 0, 2)
        prept("S", 1, 0, 3)
        weigh(0, 2, 1)
        weigh(0, 3, 0)
        weigh(0, 3, 1)
        quant_k1(2, 4)
        scores(1, 0)
        scores(1, 1)
        prept("V", 1, 2, 0)
        quant_w(0, 4, 8)
        prept("V", 1, 2, 1)
        prept("S", 1, 2, 3)
        il("S", 1, 0)
        il("G", 1, 1)
        weigh(1, 0, 0)
        weigh(1, 0, 1)
        scores(1, 2)
        prept("V", 1, 2, 2)
        pack_v("S", 0, 0)
        sigmoid(0)
        make_gate("G", 0)
        pack_v("S", 0, 1)
        weigh(1, 1, 0)
        weigh(1, 1, 1)
        scores(1, 3)
        pack_v("S", 1, 0)
        pack_v("S", 1, 1)
        sigmoid(1)
        il("S", 1, 3)
        table()
        il("V", 1, 2)
        quant_w(1, 0, 4)
        quant_v(0)
        quant_v(1)
        make_gate("G", 1)
        values(0, 0)
        values(0, 1)
        values(1, 0)
        values(1, 1)
        weigh(1, 2, 0)
        weigh(1, 2, 1)
        weigh(1, 3, 0)
        quant_w(1, 4, 6)
        values(2, 0)
        values(2, 1)
        weigh(1, 3, 1)
        quant_w(1, 6, 7)
        quant_w(1, 7, 8)
        values(3, 0)
        values(3, 1)
        square(0, 0)
        square(0, 1)
        square(1, 0)
        rsq(0, 0, 2)
        square(1, 1)
        square(2, 0)
        rsq(1, 0, 2)
        square(2, 1)
        square(3, 0)
        rsq(2, 0, 2)
        square(3, 1)
        rsq(3, 0, 2)
        make_gate("V", 2)
        finish(0, 0)
        finish(0, 1)
        store(0, 0, 2)
        make_gate("V", 3)
        finish(1, 0)
        finish(1, 1)
        store(1, 0, 2)
        finish(2, 0)
        finish(2, 1)
        store(2, 0, 2)
        finish(3, 0)
        store(3, 0, 1)
        finish(3, 1)
        store(3, 1, 2)
